import numpy as np
import ml_dtypes


def mxq(x, axis, fmt="e4m3"):
    dtype, down = {"e4m3": (ml_dtypes.float8_e4m3fn, 7), "e5m2": (ml_dtypes.float8_e5m2, 14)}[fmt]
    v = np.moveaxis(np.asarray(x, np.float32).astype(ml_dtypes.bfloat16).astype(np.float64), axis, -1)
    blocks = v.reshape(v.shape[:-1] + (-1, 32))
    amax = np.abs(blocks).max(-1, keepdims=True)
    byte = np.maximum(np.where(amax > 0, np.frexp(amax)[1] - 1 + 127, 0) - down, 1)
    scale = np.exp2(byte - 127.0)
    codes = (blocks / scale).astype(np.float32).astype(dtype).astype(np.float64)
    return np.moveaxis((codes * scale).reshape(v.shape), -1, axis)


WIDE = False


def mx_kscale(k):
    if not WIDE:
        return np.ones(k)
    levels = np.array([10, -10, 5, -5, 0])
    if k % 512:
        return np.exp2(np.random.permutation(np.resize(levels, k // 32))).repeat(32)
    a = np.empty((k // 512, 16))
    for p in range(k // 512):
        a[p, :8] = np.random.permutation(np.resize(levels, 8))
        for g in range(8):
            far = levels[np.abs(levels - a[p, g]) >= 10]
            a[p, g + 8] = far[np.random.randint(len(far))]
    return np.exp2(a.ravel()).repeat(32)


def f64(x):
    return np.asarray(x).astype(np.float64)


def striped(idx):
    return np.tile(idx.reshape(-1, 16).T, (8, 1)).astype(np.uint16)


def unstriped(offs):
    return offs[:16].T.reshape(-1).astype(np.int64)


def pack_weight(w):
    k, n = w.shape
    w = f64(np.asarray(w, np.float32).astype(ml_dtypes.bfloat16)).reshape(k // 32, 32, n)
    amax = np.abs(w).max(1)
    byte = np.clip(np.where(amax > 0, np.frexp(amax)[1] - 1 + 127 - 7, 1), 1, 254)
    scaled = (w * np.exp2(127.0 - byte)[:, None, :]).reshape(k, n).astype(np.float32)
    words = np.ascontiguousarray(scaled.reshape(k // 512, 128, 4, n).transpose(0, 1, 3, 2)).astype(ml_dtypes.float8_e4m3fn).view(np.uint8)
    return words, np.ascontiguousarray(byte.astype(np.uint8).reshape(k // 512, 16, n))


def unpack_weight(words, scales):
    g, p, n, _ = words.shape
    vals = np.ascontiguousarray(words).view(ml_dtypes.float8_e4m3fn).astype(np.float64) * np.repeat(np.exp2(scales.astype(np.float64) - 127.0), 8, axis=1)[..., None]
    return vals.transpose(0, 1, 3, 2).reshape(g * 512, n)


def sigmoid(v):
    return 1.0 / (1.0 + np.exp(-np.maximum(v, -700.0)))


K, T, S, V, H, W, G = 512, 2048, 512, 512, 512, 1024, 2048
P = 2 ** 7


def setup_inputs():
    n = np.random.standard_normal
    s = mx_kscale(K)[:, None]
    u = mx_kscale(H)
    packed_xT = pack_weight(n((K, T)) * s)
    packed_eT = pack_weight(n((K, W)) * s)
    packed_vT = pack_weight(n((H, G)) / np.sqrt(H) / u[:, None])
    return {
        "x_words": packed_xT[0],
        "x_scales": packed_xT[1],
        "e_words": packed_eT[0],
        "e_scales": packed_eT[1],
        "w1": (n((K, H)) / np.sqrt(K) / s * u).astype(np.float32),
        "w2": (n((K, H)) / np.sqrt(K) / s).astype(np.float32),
        "v_words": packed_vT[0],
        "v_scales": packed_vT[1],
        "bias": (np.tile(0.5 * np.random.standard_normal(G), (P, 1))).astype(np.float32),
        "offs": striped(np.random.permutation(T)[:S]),
        "rel": striped(np.random.permutation(W)[:S]),
        "tail": striped(np.random.permutation(G)[:V]),
    }


def reference(x_words, x_scales, e_words, e_scales, w1, w2, v_words, v_scales, bias, offs, rel, tail):
    xq = unpack_weight(x_words, x_scales)[:, unstriped(offs)]
    y = mxq(f64(w1), 0, "e4m3").T @ xq
    e_rel = unpack_weight(e_words, e_scales)[:, unstriped(rel)]
    r = np.tanh(mxq(f64(w2), 0, "e4m3").T @ e_rel)
    z = y * r
    v_tail = unpack_weight(v_words, v_scales)[:, unstriped(tail)]
    return sigmoid((mxq(z, 0, "e4m3").T @ v_tail) + f64(bias)[:1][:, unstriped(tail)])

@@ -1,0 +1,209 @@
+from contextlib import ExitStack
+
+import concourse.mybir as mybir
+from concourse.masks import make_identity
+
+K, T, S, V, H, W, G = 512, 2048, 512, 512, 512, 1024, 2048
+FLOPS = 2 * K * H * S * 2 + 2 * H * S * V
+
+F32 = mybir.dt.float32
+BF16 = mybir.dt.bfloat16
+I32 = mybir.dt.int32
+U32 = mybir.dt.uint32
+U16 = mybir.dt.uint16
+U8 = mybir.dt.uint8
+FP8X4 = mybir.dt.float8_e4m3fn_x4
+ACT = mybir.ActivationFunctionType
+ALU = mybir.AluOpType
+
+P = 128
+PACK = 4
+BLOCK = 128
+
+
+def tile_picked_zkge_tanh_p_kernel(
+    tc, x_words, x_scales, e_words, e_scales, w1, w2, v_words, v_scales, bias, offs, rel, tail, out
+):
+    nc = tc.nc
+    with ExitStack() as ctx:
+        keep = ctx.enter_context(tc.tile_pool(name="keep", bufs=1))
+        laid = ctx.enter_context(tc.tile_pool(name="laid", bufs=1))
+        psum = ctx.enter_context(tc.psum_pool(name="psum", bufs=1))
+
+        def load_list(name, src):
+            t = keep.tile([P, src.shape[1]], U16, name=name)
+            nc.sync.dma_start(t[:], src)
+            return t
+
+        def load_scales(t, src, row0):
+            nc.vector.memset(t[:].bitcast(I32), 0)
+            for q in range(4):
+                nc.sync.dma_start(
+                    t[32 * q + row0 : 32 * q + row0 + 4, :].bitcast(I32), src[0, 4 * q : 4 * q + 4, :].bitcast(I32)
+                )
+
+        def load_words(t, src):
+            nc.sync.dma_start(t[:], src[0].rearrange("p n t -> p (n t)").bitcast(I32))
+
+        def load_weight(t, src):
+            nc.sync.dma_start(t[:], src.rearrange("(p j) c -> p j c", j=PACK))
+
+        def gather(dst, window, idx):
+            nc.vector.tensor_copy(dst, window.indirect(idx))
+
+        def cast_weight(t, raw):
+            nc.scalar.copy(
+                t[:].rearrange("p (t m j) -> p m j t", t=PACK, j=PACK),
+                raw[:].rearrange("p j (m t) -> p m j t", t=PACK),
+            )
+
+        def quantize(codes, scales, values):
+            nc.vector.quantize_mx(out=codes[:].bitcast(FP8X4), scales=scales[:], in_=values[:])
+            return codes, scales
+
+        def project(bank, wq, codes, scales, row0, b):
+            cols = slice(b * BLOCK, (b + 1) * BLOCK)
+            for t in range(PACK):
+                chan = slice(t * P, (t + 1) * P)
+                nc.tensor.matmul_mx(
+                    out=bank[:, t, :],
+                    lhsT=wq[0][:, chan].bitcast(FP8X4),
+                    lhsT_scale=wq[1][:, chan],
+                    rhs=codes[:, cols].bitcast(FP8X4),
+                    rhs_scale=scales[row0:P, cols],
+                    start=True,
+                    stop=True,
+                )
+
+        E_ROW, X_ROW, V_ROW = 4, 8, 12
+
+        rel_sb = load_list("rel_sb", rel)
+        offs_sb = load_list("offs_sb", offs)
+        tail_sb = load_list("tail_sb", tail)
+        AT_W2, AT_X, AT_V, AT_W1, AT_VS, AT_W2BF, AT_W1BF = 0, 8192, 16384, 25088, 33280, 35328, 39424
+
+        LEAD = 64
+        zeros = laid.tile([P, LEAD], F32, offset=AT_W2, align_bytes=64)
+        nc.vector.memset(zeros[:], 0.0)
+        zeros_end = laid.tile([P, LEAD], F32, offset=AT_W1, align_bytes=64)
+        nc.vector.memset(zeros_end[:], 0.0)
+        ident = keep.tile([P, P], F32)
+        make_identity(nc, ident[:])
+
+        e_sc = keep.tile([P, W], U8, tag="e_slot", align_bytes=64)
+        load_scales(e_sc, e_scales, E_ROW)
+        bias_tab = laid.tile([P, G], F32, offset=AT_V, align_bytes=64)
+        nc.vector.tensor_copy(bias_tab[:, 0:LEAD], zeros[:])
+        w2_raw = laid.tile([P, PACK, H], F32, offset=AT_W2, align_bytes=64)
+        load_weight(w2_raw, w2)
+        warm = keep.tile([P, 8], F32)
+        nc.scalar.activation(warm[64:P, :], bias_tab[64:P, 0:8], ACT.Sigmoid)
+
+        x_sc = laid.tile([P, T], U8, offset=AT_X, align_bytes=64)
+        load_scales(x_sc, x_scales, X_ROW)
+        nc.vector.memset(bias_tab[:, LEAD : G - LEAD], 0.0)
+        nc.vector.tensor_copy(bias_tab[:, G - LEAD : G], zeros_end[:])
+        nc.sync.dma_start(bias_tab[0:1, :], bias[0:1, :])
+        w1_raw = laid.tile([P, PACK, H], F32, offset=AT_W1, align_bytes=64)
+        load_weight(w1_raw, w1)
+        v_sc = laid.tile([P, G], U8, offset=AT_VS, align_bytes=64)
+        load_scales(v_sc, v_scales, V_ROW)
+
+        e_s = keep.tile([P, S], U8, align_bytes=64)
+        gather(e_s[:], e_sc[:], rel_sb[:])
+        e_tab = keep.tile([P, W], I32, tag="e_slot", align_bytes=64)
+        load_words(e_tab, e_words)
+        x_s = keep.tile([P, S], U8, align_bytes=64)
+        gather(x_s[:], x_sc[:], offs_sb[:])
+        x_tab = laid.tile([P, T], I32, offset=AT_X, align_bytes=64)
+        load_words(x_tab, x_words)
+        bias_row = keep.tile([P, V], F32)
+        gather(bias_row[:], bias_tab[:], tail_sb[:])
+        v_tab = laid.tile([P, G], I32, offset=AT_V + H, align_bytes=64)
+        load_words(v_tab, v_words)
+        w2_bf = laid.tile([P, PACK * H], BF16, offset=AT_W2BF, align_bytes=64)
+        cast_weight(w2_bf, w2_raw)
+        w1_bf = laid.tile([P, PACK * H], BF16, offset=AT_W1BF, align_bytes=64)
+        cast_weight(w1_bf, w1_raw)
+        w2_codes = keep.tile([P, H], U32, align_bytes=64)
+        w2_scales = laid.tile([P, H], U8, offset=AT_V, align_bytes=64)
+        w2_q = quantize(w2_codes, w2_scales, w2_bf)
+        v_s = laid.tile([P, V], U8, offset=AT_W2BF + 4 * S, align_bytes=64)
+        gather(v_s[:], v_sc[:], tail_sb[:])
+        e_q = laid.tile([P, S], U32, offset=AT_W2BF, align_bytes=64)
+        gather(e_q[:], e_tab[:].bitcast(U32), rel_sb[:])
+
+        turned = psum.tile([P, V], F32, name="turned", tag="obank", bufs=2)
+        for c in range(V // P):
+            nc.tensor.transpose(turned[:, c * P : (c + 1) * P], bias_row[:, c * P : (c + 1) * P], ident[:])
+        bias_col = laid.tile([P, V // P], F32, offset=AT_W1, align_bytes=64)
+        nc.scalar.copy(bias_col[:], turned[:, 0:V:P])
+        spread = psum.tile([P, V], F32, name="spread", tag="obank", bufs=2)
+        for c in range(V // P):
+            nc.tensor.transpose(spread[:, c * P : (c + 1) * P], bias_col[:, c : c + 1].to_broadcast([P, P]), ident[:])
+        bias_g = keep.tile([P, V], F32)
+        nc.scalar.copy(bias_g[:], spread[:])
+
+        n_blocks = S // BLOCK
+        r_banks = []
+        for b in range(n_blocks):
+            r_bank = psum.tile([P, PACK, BLOCK], F32, name="r_bank", tag="rbank", bufs=4)
+            project(r_bank, w2_q, e_q, e_s, E_ROW, b)
+            r_banks.append(r_bank)
+
+        r_sb = []
+        for b in range(n_blocks):
+            r_b = keep.tile([P, BLOCK, PACK], F32, name="r%d" % b)
+            nc.scalar.activation(r_b[:], r_banks[b][:].rearrange("p t n -> p n t"), ACT.Tanh)
+            r_sb.append(r_b)
+
+        w1_codes = keep.tile([P, H], U32, tag="e_slot", align_bytes=64)
+        w1_scales = keep.tile([P, H], U8, align_bytes=64)
+        w1_q = quantize(w1_codes, w1_scales, w1_bf)
+        x_q = laid.tile([P, S], U32, offset=AT_W1BF, align_bytes=64)
+        for h in range(2):
+            gather(x_q[:, h * S // 2 : (h + 1) * S // 2], x_tab[:].bitcast(U32), offs_sb[:, h * S // 32 : (h + 1) * S // 32])
+
+        def product(b):
+            y_bank = psum.tile([P, PACK, BLOCK], F32, name="y_bank", tag="ybank", bufs=2)
+            project(y_bank, w1_q, x_q, x_s, X_ROW, b)
+            z_b = keep.tile([P, BLOCK * PACK], BF16, name="z%d" % b, tag="z%d" % b, align_bytes=64)
+            nc.vector.tensor_tensor(
+                z_b[:].rearrange("p (n t) -> p n t", t=PACK), y_bank[:].rearrange("p t n -> p n t"), r_sb[b][:], ALU.mult
+            )
+            return z_b
+
+        def quantize_z(b, z_b):
+            z_codes = keep.tile([P, BLOCK], U32, name="z_codes%d" % b, align_bytes=64)
+            z_scales = keep.tile([P, BLOCK], U8, name="z_scales%d" % b, align_bytes=64)
+            return quantize(z_codes, z_scales, z_b)
+
+        def score(b, z_q, v_q):
+            o_bank = psum.tile([P, V], F32, name="o_bank", tag="obank", bufs=2)
+            nc.tensor.matmul_mx(
+                out=o_bank[:],
+                lhsT=z_q[0][:].bitcast(FP8X4),
+                lhsT_scale=z_q[1][:],
+                rhs=v_q[:].bitcast(FP8X4),
+                rhs_scale=v_s[V_ROW:P, :],
+                start=True,
+                stop=True,
+            )
+            logit = keep.tile([P, V], F32, name="logit%d" % b)
+            nc.vector.tensor_tensor(logit[:], o_bank[:], bias_g[:], ALU.add)
+            prob = keep.tile([P, V], F32, name="prob%d" % b)
+            nc.scalar.activation(prob[:], logit[:], ACT.Sigmoid)
+            nc.sync.dma_start(out[b * BLOCK : (b + 1) * BLOCK, :], prob[:])
+
+        z_bf = [product(0), product(1)]
+        z_qs = [quantize_z(0, z_bf[0])]
+        v_q = keep.tile([P, V], U32, tag="z0", align_bytes=64)
+        gather(v_q[:], v_tab[:].bitcast(U32), tail_sb[:])
+        for b in range(1, n_blocks):
+            if b + 1 < n_blocks:
+                z_bf.append(product(b + 1))
+            else:
+                score(0, z_qs[0], v_q)
+            z_qs.append(quantize_z(b, z_bf[b]))
+        for b in range(1, n_blocks):
+            score(b, z_qs[b], v_q)

@@ -37,10 +37,8 @@ def tile_picked_zkge_tanh_p_kernel(
 
         def load_scales(t, src, row0):
             nc.vector.memset(t[:].bitcast(I32), 0)
-            for q in range(4):
-                nc.sync.dma_start(
-                    t[32 * q + row0 : 32 * q + row0 + 4, :].bitcast(I32), src[0, 4 * q : 4 * q + 4, :].bitcast(I32)
-                )
+            for r in range(4):
+                nc.sync.dma_start(t[row0 + r : P : 32, :].bitcast(I32), src[0, r:16:4, :].bitcast(I32))
 
         def load_words(t, src):
             nc.sync.dma_start(t[:], src[0].rearrange("p n t -> p (n t)").bitcast(I32))
@@ -53,8 +51,8 @@ def tile_picked_zkge_tanh_p_kernel(
 
         def cast_weight(t, raw):
             nc.scalar.copy(
-                t[:].rearrange("p (t m j) -> p m j t", t=PACK, j=PACK),
-                raw[:].rearrange("p j (m t) -> p m j t", t=PACK),
+                t[:].rearrange("p (t m j) -> p m t j", t=PACK, j=PACK),
+                raw[:].rearrange("p j (m t) -> p m t j", t=PACK),
             )
 
         def quantize(codes, scales, values):
@@ -80,28 +78,33 @@ def tile_picked_zkge_tanh_p_kernel(
         rel_sb = load_list("rel_sb", rel)
         offs_sb = load_list("offs_sb", offs)
         tail_sb = load_list("tail_sb", tail)
-        AT_W2, AT_X, AT_V, AT_W1, AT_VS, AT_W2BF, AT_W1BF = 0, 8192, 16384, 25088, 33280, 35328, 39424
+        AT_W2, AT_X, AT_V, AT_W1, AT_BIAS, AT_W2BF, AT_W1BF, AT_VS = 0, 8192, 16896, 26112, 34304, 42496, 46592, 50688
 
         LEAD = 64
         zeros = laid.tile([P, LEAD], F32, offset=AT_W2, align_bytes=64)
         nc.vector.memset(zeros[:], 0.0)
-        zeros_end = laid.tile([P, LEAD], F32, offset=AT_W1, align_bytes=64)
-        nc.vector.memset(zeros_end[:], 0.0)
         ident = keep.tile([P, P], F32)
         make_identity(nc, ident[:])
 
-        e_sc = keep.tile([P, W], U8, tag="e_slot", align_bytes=64)
+        e_sc = keep.tile([P, W], U8, align_bytes=64)
         load_scales(e_sc, e_scales, E_ROW)
-        bias_tab = laid.tile([P, G], F32, offset=AT_V, align_bytes=64)
+        bias_tab = laid.tile([P, G], F32, offset=AT_BIAS, align_bytes=64)
         nc.vector.tensor_copy(bias_tab[:, 0:LEAD], zeros[:])
         w2_raw = laid.tile([P, PACK, H], F32, offset=AT_W2, align_bytes=64)
         load_weight(w2_raw, w2)
         warm = keep.tile([P, 8], F32)
         nc.scalar.activation(warm[64:P, :], bias_tab[64:P, 0:8], ACT.Sigmoid)
 
+        zeros_mid = laid.tile([P, LEAD], F32, offset=AT_V - H, align_bytes=64)
+        nc.vector.memset(zeros_mid[:], 0.0)
+        zeros_end = laid.tile([P, LEAD], F32, offset=AT_W1, align_bytes=64)
+        nc.vector.memset(zeros_end[:], 0.0)
         x_sc = laid.tile([P, T], U8, offset=AT_X, align_bytes=64)
         load_scales(x_sc, x_scales, X_ROW)
-        nc.vector.memset(bias_tab[:, LEAD : G - LEAD], 0.0)
+        nc.vector.tensor_copy(bias_tab[:, LEAD : 2 * LEAD], zeros_mid[:])
+        e_tab = laid.tile([P, W], I32, offset=AT_V - H, align_bytes=64)
+        load_words(e_tab, e_words)
+        nc.vector.memset(bias_tab[:, 2 * LEAD : G - LEAD], 0.0)
         nc.vector.tensor_copy(bias_tab[:, G - LEAD : G], zeros_end[:])
         nc.sync.dma_start(bias_tab[0:1, :], bias[0:1, :])
         w1_raw = laid.tile([P, PACK, H], F32, offset=AT_W1, align_bytes=64)
@@ -111,38 +114,25 @@ def tile_picked_zkge_tanh_p_kernel(
 
         e_s = keep.tile([P, S], U8, align_bytes=64)
         gather(e_s[:], e_sc[:], rel_sb[:])
-        e_tab = keep.tile([P, W], I32, tag="e_slot", align_bytes=64)
-        load_words(e_tab, e_words)
         x_s = keep.tile([P, S], U8, align_bytes=64)
         gather(x_s[:], x_sc[:], offs_sb[:])
         x_tab = laid.tile([P, T], I32, offset=AT_X, align_bytes=64)
         load_words(x_tab, x_words)
-        bias_row = keep.tile([P, V], F32)
-        gather(bias_row[:], bias_tab[:], tail_sb[:])
-        v_tab = laid.tile([P, G], I32, offset=AT_V + H, align_bytes=64)
+        e_q = keep.tile([P, S], U32, align_bytes=64)
+        gather(e_q[:], e_tab[:].bitcast(U32), rel_sb[:])
+        v_tab = laid.tile([P, G], I32, offset=AT_V, align_bytes=64)
         load_words(v_tab, v_words)
         w2_bf = laid.tile([P, PACK * H], BF16, offset=AT_W2BF, align_bytes=64)
         cast_weight(w2_bf, w2_raw)
         w1_bf = laid.tile([P, PACK * H], BF16, offset=AT_W1BF, align_bytes=64)
         cast_weight(w1_bf, w1_raw)
         w2_codes = keep.tile([P, H], U32, align_bytes=64)
-        w2_scales = laid.tile([P, H], U8, offset=AT_V, align_bytes=64)
+        w2_scales = laid.tile([P, H], U8, offset=AT_V - H, align_bytes=64)
         w2_q = quantize(w2_codes, w2_scales, w2_bf)
-        v_s = laid.tile([P, V], U8, offset=AT_W2BF + 4 * S, align_bytes=64)
+        bias_row = keep.tile([P, V], F32)
+        gather(bias_row[:], bias_tab[:], tail_sb[:])
+        v_s = laid.tile([P, V], U8, offset=AT_W2BF - V // 2, align_bytes=64)
         gather(v_s[:], v_sc[:], tail_sb[:])
-        e_q = laid.tile([P, S], U32, offset=AT_W2BF, align_bytes=64)
-        gather(e_q[:], e_tab[:].bitcast(U32), rel_sb[:])
-
-        turned = psum.tile([P, V], F32, name="turned", tag="obank", bufs=2)
-        for c in range(V // P):
-            nc.tensor.transpose(turned[:, c * P : (c + 1) * P], bias_row[:, c * P : (c + 1) * P], ident[:])
-        bias_col = laid.tile([P, V // P], F32, offset=AT_W1, align_bytes=64)
-        nc.scalar.copy(bias_col[:], turned[:, 0:V:P])
-        spread = psum.tile([P, V], F32, name="spread", tag="obank", bufs=2)
-        for c in range(V // P):
-            nc.tensor.transpose(spread[:, c * P : (c + 1) * P], bias_col[:, c : c + 1].to_broadcast([P, P]), ident[:])
-        bias_g = keep.tile([P, V], F32)
-        nc.scalar.copy(bias_g[:], spread[:])
 
         n_blocks = S // BLOCK
         r_banks = []
@@ -151,14 +141,25 @@ def tile_picked_zkge_tanh_p_kernel(
             project(r_bank, w2_q, e_q, e_s, E_ROW, b)
             r_banks.append(r_bank)
 
+        turned = psum.tile([P, V], F32, name="turned", tag="bbank", bufs=2)
+        for c in range(V // P):
+            nc.tensor.transpose(turned[:, c * P : (c + 1) * P], bias_row[:, c * P : (c + 1) * P], ident[:])
+        bias_col = laid.tile([P, V // P], F32, offset=AT_W1 + 7168, align_bytes=64)
+        nc.scalar.copy(bias_col[:], turned[:, 0:V:P])
+        spread = psum.tile([P, V], F32, name="spread", tag="bbank", bufs=2)
+        for c in range(V // P):
+            nc.tensor.transpose(spread[:, c * P : (c + 1) * P], bias_col[:, c : c + 1].to_broadcast([P, P]), ident[:])
+
         r_sb = []
         for b in range(n_blocks):
-            r_b = keep.tile([P, BLOCK, PACK], F32, name="r%d" % b)
+            r_b = laid.tile([P, BLOCK, PACK], F32, name="r%d" % b, offset=AT_W1 - 1024 + b * 4 * BLOCK * PACK, align_bytes=64)
             nc.scalar.activation(r_b[:], r_banks[b][:].rearrange("p t n -> p n t"), ACT.Tanh)
             r_sb.append(r_b)
+        bias_g = keep.tile([P, V], F32)
+        nc.scalar.copy(bias_g[:], spread[:])
 
-        w1_codes = keep.tile([P, H], U32, tag="e_slot", align_bytes=64)
-        w1_scales = keep.tile([P, H], U8, align_bytes=64)
+        w1_codes = laid.tile([P, H], U32, offset=AT_BIAS, align_bytes=64)
+        w1_scales = laid.tile([P, H], U8, offset=AT_VS, align_bytes=64)
         w1_q = quantize(w1_codes, w1_scales, w1_bf)
         x_q = laid.tile([P, S], U32, offset=AT_W1BF, align_bytes=64)
         for h in range(2):
@@ -167,7 +168,10 @@ def tile_picked_zkge_tanh_p_kernel(
         def product(b):
             y_bank = psum.tile([P, PACK, BLOCK], F32, name="y_bank", tag="ybank", bufs=2)
             project(y_bank, w1_q, x_q, x_s, X_ROW, b)
-            z_b = keep.tile([P, BLOCK * PACK], BF16, name="z%d" % b, tag="z%d" % b, align_bytes=64)
+            if b == n_blocks - 1:
+                z_b = laid.tile([P, BLOCK * PACK], BF16, name="z_last", offset=AT_V + 4 * W, align_bytes=64)
+            else:
+                z_b = keep.tile([P, BLOCK * PACK], BF16, name="z%d" % b, align_bytes=64)
             nc.vector.tensor_tensor(
                 z_b[:].rearrange("p (n t) -> p n t", t=PACK), y_bank[:].rearrange("p t n -> p n t"), r_sb[b][:], ALU.mult
             )
@@ -179,7 +183,7 @@ def tile_picked_zkge_tanh_p_kernel(
             return quantize(z_codes, z_scales, z_b)
 
         def score(b, z_q, v_q):
-            o_bank = psum.tile([P, V], F32, name="o_bank", tag="obank", bufs=2)
+            o_bank = psum.tile([P, V], F32, name="o_bank", tag="rbank", bufs=4)
             nc.tensor.matmul_mx(
                 out=o_bank[:],
                 lhsT=z_q[0][:].bitcast(FP8X4),
@@ -190,20 +194,24 @@ def tile_picked_zkge_tanh_p_kernel(
                 stop=True,
             )
             logit = keep.tile([P, V], F32, name="logit%d" % b)
-            nc.vector.tensor_tensor(logit[:], o_bank[:], bias_g[:], ALU.add)
             prob = keep.tile([P, V], F32, name="prob%d" % b)
-            nc.scalar.activation(prob[:], logit[:], ACT.Sigmoid)
-            nc.sync.dma_start(out[b * BLOCK : (b + 1) * BLOCK, :], prob[:])
+            width = V // 2 if b == n_blocks - 1 else V
+            for c0 in range(0, V, width):
+                cols = slice(c0, c0 + width)
+                nc.vector.tensor_tensor(logit[:, cols], o_bank[:, cols], bias_g[:, cols], ALU.add)
+                nc.scalar.activation(prob[:, cols], logit[:, cols], ACT.Sigmoid)
+                nc.sync.dma_start(out[b * BLOCK : (b + 1) * BLOCK, cols], prob[:, cols])
 
-        z_bf = [product(0), product(1)]
-        z_qs = [quantize_z(0, z_bf[0])]
-        v_q = keep.tile([P, V], U32, tag="z0", align_bytes=64)
+        z_bf = [product(0)]
+        z_qs = []
+        for b in range(1, n_blocks - 1):
+            z_bf.append(product(b))
+            z_qs.append(quantize_z(b - 1, z_bf[b - 1]))
+        v_q = keep.tile([P, V], U32, align_bytes=64)
         gather(v_q[:], v_tab[:].bitcast(U32), tail_sb[:])
-        for b in range(1, n_blocks):
-            if b + 1 < n_blocks:
-                z_bf.append(product(b + 1))
-            else:
-                score(0, z_qs[0], v_q)
-            z_qs.append(quantize_z(b, z_bf[b]))
+        z_qs.append(quantize_z(n_blocks - 2, z_bf[n_blocks - 2]))
+        z_bf.append(product(n_blocks - 1))
+        score(0, z_qs[0], v_q)
+        z_qs.append(quantize_z(n_blocks - 1, z_bf[n_blocks - 1]))
         for b in range(1, n_blocks):
             score(b, z_qs[b], v_q)

@@ -27,7 +27,6 @@ def tile_picked_zkge_tanh_p_kernel(
     nc = tc.nc
     with ExitStack() as ctx:
         keep = ctx.enter_context(tc.tile_pool(name="keep", bufs=1))
-        laid = ctx.enter_context(tc.tile_pool(name="laid", bufs=1))
         psum = ctx.enter_context(tc.psum_pool(name="psum", bufs=1))
 
         def load_list(name, src):
@@ -35,10 +34,21 @@ def tile_picked_zkge_tanh_p_kernel(
             nc.sync.dma_start(t[:], src)
             return t
 
-        def load_scales(t, src, row0):
+        def load_scales(name, src, first):
+            t = keep.tile([P, src.shape[2]], U8, name=name, align_bytes=64)
             nc.vector.memset(t[:].bitcast(I32), 0)
-            for r in range(4):
-                nc.sync.dma_start(t[row0 + r : P : 32, :].bitcast(I32), src[0, r:16:4, :].bitcast(I32))
+            nc.sync.dma_start(t[first : first + 16, :].bitcast(I32), src[0].bitcast(I32))
+            return t
+
+        def cleared_plane(name):
+            t = keep.tile([P, S], U8, name=name, align_bytes=64)
+            nc.vector.memset(t[:].bitcast(I32), 0)
+            return t
+
+        def place_scales(plane, picked, first):
+            for q in range(4):
+                rows = picked[first + 4 * q : first + 4 * q + 4, :]
+                nc.sync.dma_start(plane[32 * q : 32 * q + 4, :].bitcast(I32), rows.bitcast(I32))
 
         def load_words(t, src):
             nc.sync.dma_start(t[:], src[0].rearrange("p n t -> p (n t)").bitcast(I32))
@@ -49,17 +59,17 @@ def tile_picked_zkge_tanh_p_kernel(
         def gather(dst, window, idx):
             nc.vector.tensor_copy(dst, window.indirect(idx))
 
-        def cast_weight(t, raw):
-            nc.scalar.copy(
-                t[:].rearrange("p (t m j) -> p m t j", t=PACK, j=PACK),
-                raw[:].rearrange("p j (m t) -> p m t j", t=PACK),
+        def cast_weight(copy, t, raw, m0, m1):
+            copy(
+                t[:].rearrange("p (t m j) -> p m t j", t=PACK, j=PACK)[:, m0:m1],
+                raw[:].rearrange("p j (m t) -> p m t j", t=PACK)[:, m0:m1],
             )
 
         def quantize(codes, scales, values):
             nc.vector.quantize_mx(out=codes[:].bitcast(FP8X4), scales=scales[:], in_=values[:])
             return codes, scales
 
-        def project(bank, wq, codes, scales, row0, b):
+        def project(bank, wq, codes, scales, b):
             cols = slice(b * BLOCK, (b + 1) * BLOCK)
             for t in range(PACK):
                 chan = slice(t * P, (t + 1) * P)
@@ -68,108 +78,93 @@ def tile_picked_zkge_tanh_p_kernel(
                     lhsT=wq[0][:, chan].bitcast(FP8X4),
                     lhsT_scale=wq[1][:, chan],
                     rhs=codes[:, cols].bitcast(FP8X4),
-                    rhs_scale=scales[row0:P, cols],
+                    rhs_scale=scales[:, cols],
                     start=True,
                     stop=True,
                 )
 
-        E_ROW, X_ROW, V_ROW = 4, 8, 12
+        E_ROW, X_ROW, V_ROW = 0, 16, 64
 
         rel_sb = load_list("rel_sb", rel)
         offs_sb = load_list("offs_sb", offs)
         tail_sb = load_list("tail_sb", tail)
-        AT_W2, AT_X, AT_V, AT_W1, AT_BIAS, AT_W2BF, AT_W1BF, AT_VS = 0, 8192, 16896, 26112, 34304, 42496, 46592, 50688
+        e_sc = load_scales("e_sc", e_scales, E_ROW)
+        x_sc = load_scales("x_sc", x_scales, X_ROW)
+        v_sc = load_scales("v_sc", v_scales, V_ROW)
+        w2_raw = keep.tile([P, PACK, H], F32, align_bytes=64)
+        load_weight(w2_raw, w2)
+        e_tab = keep.tile([P, W], I32, align_bytes=64)
+        load_words(e_tab, e_words)
+        bias_tab = keep.tile([P, G], F32, align_bytes=64)
+        nc.vector.memset(bias_tab[:], 0.0)
+        nc.sync.dma_start(bias_tab[0:1, :], bias[0:1, :])
+        w1_raw = keep.tile([P, PACK, H], F32, align_bytes=64)
+        load_weight(w1_raw, w1)
 
-        LEAD = 64
-        zeros = laid.tile([P, LEAD], F32, offset=AT_W2, align_bytes=64)
-        nc.vector.memset(zeros[:], 0.0)
         ident = keep.tile([P, P], F32)
         make_identity(nc, ident[:])
-
-        e_sc = keep.tile([P, W], U8, align_bytes=64)
-        load_scales(e_sc, e_scales, E_ROW)
-        bias_tab = laid.tile([P, G], F32, offset=AT_BIAS, align_bytes=64)
-        nc.vector.tensor_copy(bias_tab[:, 0:LEAD], zeros[:])
-        w2_raw = laid.tile([P, PACK, H], F32, offset=AT_W2, align_bytes=64)
-        load_weight(w2_raw, w2)
         warm = keep.tile([P, 8], F32)
         nc.scalar.activation(warm[64:P, :], bias_tab[64:P, 0:8], ACT.Sigmoid)
-
-        zeros_mid = laid.tile([P, LEAD], F32, offset=AT_V - H, align_bytes=64)
-        nc.vector.memset(zeros_mid[:], 0.0)
-        zeros_end = laid.tile([P, LEAD], F32, offset=AT_W1, align_bytes=64)
-        nc.vector.memset(zeros_end[:], 0.0)
-        x_sc = laid.tile([P, T], U8, offset=AT_X, align_bytes=64)
-        load_scales(x_sc, x_scales, X_ROW)
-        nc.vector.tensor_copy(bias_tab[:, LEAD : 2 * LEAD], zeros_mid[:])
-        e_tab = laid.tile([P, W], I32, offset=AT_V - H, align_bytes=64)
-        load_words(e_tab, e_words)
-        nc.vector.memset(bias_tab[:, 2 * LEAD : G - LEAD], 0.0)
-        nc.vector.tensor_copy(bias_tab[:, G - LEAD : G], zeros_end[:])
-        nc.sync.dma_start(bias_tab[0:1, :], bias[0:1, :])
-        w1_raw = laid.tile([P, PACK, H], F32, offset=AT_W1, align_bytes=64)
-        load_weight(w1_raw, w1)
-        v_sc = laid.tile([P, G], U8, offset=AT_VS, align_bytes=64)
-        load_scales(v_sc, v_scales, V_ROW)
+        e_plane = cleared_plane("e_plane")
+        x_plane = cleared_plane("x_plane")
+        v_plane = cleared_plane("v_plane")
 
         e_s = keep.tile([P, S], U8, align_bytes=64)
         gather(e_s[:], e_sc[:], rel_sb[:])
+        place_scales(e_plane, e_s, E_ROW)
+        x_tab = keep.tile([P, T], I32, align_bytes=64)
+        load_words(x_tab, x_words)
         x_s = keep.tile([P, S], U8, align_bytes=64)
         gather(x_s[:], x_sc[:], offs_sb[:])
-        x_tab = laid.tile([P, T], I32, offset=AT_X, align_bytes=64)
-        load_words(x_tab, x_words)
+        place_scales(x_plane, x_s, X_ROW)
+        v_tab = keep.tile([P, G], I32, tag="v_slot", align_bytes=64)
+        load_words(v_tab, v_words)
+        v_s = keep.tile([P, V], U8, align_bytes=64)
+        gather(v_s[:], v_sc[:], tail_sb[:])
+        place_scales(v_plane, v_s, V_ROW)
+
         e_q = keep.tile([P, S], U32, align_bytes=64)
         gather(e_q[:], e_tab[:].bitcast(U32), rel_sb[:])
-        v_tab = laid.tile([P, G], I32, offset=AT_V, align_bytes=64)
-        load_words(v_tab, v_words)
-        w2_bf = laid.tile([P, PACK * H], BF16, offset=AT_W2BF, align_bytes=64)
-        cast_weight(w2_bf, w2_raw)
-        w1_bf = laid.tile([P, PACK * H], BF16, offset=AT_W1BF, align_bytes=64)
-        cast_weight(w1_bf, w1_raw)
+        w2_bf = keep.tile([P, PACK * H], BF16, align_bytes=64)
+        cast_weight(nc.scalar.copy, w2_bf, w2_raw, 0, P)
         w2_codes = keep.tile([P, H], U32, align_bytes=64)
-        w2_scales = laid.tile([P, H], U8, offset=AT_V - H, align_bytes=64)
+        w2_scales = keep.tile([P, H], U8, align_bytes=64)
         w2_q = quantize(w2_codes, w2_scales, w2_bf)
         bias_row = keep.tile([P, V], F32)
         gather(bias_row[:], bias_tab[:], tail_sb[:])
-        v_s = laid.tile([P, V], U8, offset=AT_W2BF - V // 2, align_bytes=64)
-        gather(v_s[:], v_sc[:], tail_sb[:])
+
+        ON_VECTOR = 48
+        w1_bf = keep.tile([P, PACK * H], BF16, align_bytes=64)
+        cast_weight(nc.scalar.copy, w1_bf, w1_raw, ON_VECTOR, P)
+        cast_weight(nc.vector.tensor_copy, w1_bf, w1_raw, 0, ON_VECTOR)
+        w1_codes = keep.tile([P, H], U32, align_bytes=64)
+        w1_scales = keep.tile([P, H], U8, align_bytes=64)
+        w1_q = quantize(w1_codes, w1_scales, w1_bf)
 
         n_blocks = S // BLOCK
-        r_banks = []
-        for b in range(n_blocks):
-            r_bank = psum.tile([P, PACK, BLOCK], F32, name="r_bank", tag="rbank", bufs=4)
-            project(r_bank, w2_q, e_q, e_s, E_ROW, b)
-            r_banks.append(r_bank)
-
-        turned = psum.tile([P, V], F32, name="turned", tag="bbank", bufs=2)
-        for c in range(V // P):
-            nc.tensor.transpose(turned[:, c * P : (c + 1) * P], bias_row[:, c * P : (c + 1) * P], ident[:])
-        bias_col = laid.tile([P, V // P], F32, offset=AT_W1 + 7168, align_bytes=64)
-        nc.scalar.copy(bias_col[:], turned[:, 0:V:P])
-        spread = psum.tile([P, V], F32, name="spread", tag="bbank", bufs=2)
-        for c in range(V // P):
-            nc.tensor.transpose(spread[:, c * P : (c + 1) * P], bias_col[:, c : c + 1].to_broadcast([P, P]), ident[:])
-
         r_sb = []
         for b in range(n_blocks):
-            r_b = laid.tile([P, BLOCK, PACK], F32, name="r%d" % b, offset=AT_W1 - 1024 + b * 4 * BLOCK * PACK, align_bytes=64)
-            nc.scalar.activation(r_b[:], r_banks[b][:].rearrange("p t n -> p n t"), ACT.Tanh)
+            r_bank = psum.tile([P, PACK, BLOCK], F32, name="r_bank", tag="rbank", bufs=4)
+            project(r_bank, w2_q, e_q, e_plane, b)
+            r_b = keep.tile([P, BLOCK, PACK], F32, name="r%d" % b, align_bytes=64)
+            nc.scalar.activation(r_b[:], r_bank[:].rearrange("p t n -> p n t"), ACT.Tanh)
             r_sb.append(r_b)
-        bias_g = keep.tile([P, V], F32)
-        nc.scalar.copy(bias_g[:], spread[:])
 
-        w1_codes = laid.tile([P, H], U32, offset=AT_BIAS, align_bytes=64)
-        w1_scales = laid.tile([P, H], U8, offset=AT_VS, align_bytes=64)
-        w1_q = quantize(w1_codes, w1_scales, w1_bf)
-        x_q = laid.tile([P, S], U32, offset=AT_W1BF, align_bytes=64)
+        turned = psum.tile([P, V], F32, name="turned", tag="rbank", bufs=4)
+        for c in range(V // P):
+            nc.tensor.transpose(turned[:, c * P : (c + 1) * P], bias_row[:, c * P : (c + 1) * P], ident[:])
+        bias_col = keep.tile([P, V // P], F32)
+        nc.scalar.copy(bias_col[:], turned[:, 0:V:P])
+
+        x_q = keep.tile([P, S], U32, align_bytes=64)
         for h in range(2):
             gather(x_q[:, h * S // 2 : (h + 1) * S // 2], x_tab[:].bitcast(U32), offs_sb[:, h * S // 32 : (h + 1) * S // 32])
 
         def product(b):
-            y_bank = psum.tile([P, PACK, BLOCK], F32, name="y_bank", tag="ybank", bufs=2)
-            project(y_bank, w1_q, x_q, x_s, X_ROW, b)
+            y_bank = psum.tile([P, PACK, BLOCK], F32, name="y_bank", tag="ybank", bufs=3)
+            project(y_bank, w1_q, x_q, x_plane, b)
             if b == n_blocks - 1:
-                z_b = laid.tile([P, BLOCK * PACK], BF16, name="z_last", offset=AT_V + 4 * W, align_bytes=64)
+                z_b = keep.tile([P, BLOCK * PACK], BF16, name="z_last", tag="v_slot", align_bytes=64)
             else:
                 z_b = keep.tile([P, BLOCK * PACK], BF16, name="z%d" % b, align_bytes=64)
             nc.vector.tensor_tensor(
@@ -189,7 +184,7 @@ def tile_picked_zkge_tanh_p_kernel(
                 lhsT=z_q[0][:].bitcast(FP8X4),
                 lhsT_scale=z_q[1][:],
                 rhs=v_q[:].bitcast(FP8X4),
-                rhs_scale=v_s[V_ROW:P, :],
+                rhs_scale=v_plane[:],
                 start=True,
                 stop=True,
             )
@@ -207,6 +202,11 @@ def tile_picked_zkge_tanh_p_kernel(
         for b in range(1, n_blocks - 1):
             z_bf.append(product(b))
             z_qs.append(quantize_z(b - 1, z_bf[b - 1]))
+        spread = psum.tile([P, V], F32, name="spread", tag="ybank", bufs=3)
+        for c in range(V // P):
+            nc.tensor.transpose(spread[:, c * P : (c + 1) * P], bias_col[:, c : c + 1].to_broadcast([P, P]), ident[:])
+        bias_g = keep.tile([P, V], F32)
+        nc.scalar.copy(bias_g[:], spread[:])
         v_q = keep.tile([P, V], U32, align_bytes=64)
         gather(v_q[:], v_tab[:].bitcast(U32), tail_sb[:])
         z_qs.append(quantize_z(n_blocks - 2, z_bf[n_blocks - 2]))

@@ -27,6 +27,7 @@ def tile_picked_zkge_tanh_p_kernel(
     nc = tc.nc
     with ExitStack() as ctx:
         keep = ctx.enter_context(tc.tile_pool(name="keep", bufs=1))
+        laid = ctx.enter_context(tc.tile_pool(name="laid", bufs=1))
         psum = ctx.enter_context(tc.psum_pool(name="psum", bufs=1))
 
         def load_list(name, src):
@@ -98,8 +99,6 @@ def tile_picked_zkge_tanh_p_kernel(
         bias_tab = keep.tile([P, G], F32, align_bytes=64)
         nc.vector.memset(bias_tab[:], 0.0)
         nc.sync.dma_start(bias_tab[0:1, :], bias[0:1, :])
-        w1_raw = keep.tile([P, PACK, H], F32, align_bytes=64)
-        load_weight(w1_raw, w1)
 
         ident = keep.tile([P, P], F32)
         make_identity(nc, ident[:])
@@ -112,6 +111,8 @@ def tile_picked_zkge_tanh_p_kernel(
         e_s = keep.tile([P, S], U8, align_bytes=64)
         gather(e_s[:], e_sc[:], rel_sb[:])
         place_scales(e_plane, e_s, E_ROW)
+        w1_raw = laid.tile([P, PACK, H], F32, offset=0, align_bytes=64)
+        load_weight(w1_raw, w1)
         x_tab = keep.tile([P, T], I32, align_bytes=64)
         load_words(x_tab, x_words)
         x_s = keep.tile([P, S], U8, align_bytes=64)
@@ -146,7 +147,7 @@ def tile_picked_zkge_tanh_p_kernel(
         for b in range(n_blocks):
             r_bank = psum.tile([P, PACK, BLOCK], F32, name="r_bank", tag="rbank", bufs=4)
             project(r_bank, w2_q, e_q, e_plane, b)
-            r_b = keep.tile([P, BLOCK, PACK], F32, name="r%d" % b, align_bytes=64)
+            r_b = laid.tile([P, BLOCK, PACK], F32, name="r%d" % b, offset=b * 4 * BLOCK * PACK, align_bytes=64)
             nc.scalar.activation(r_b[:], r_bank[:].rearrange("p t n -> p n t"), ACT.Tanh)
             r_sb.append(r_b)
 

from contextlib import ExitStack

import concourse.mybir as mybir
from concourse.masks import make_identity

K, T, S, V, H, W, G = 512, 2048, 512, 512, 512, 1024, 2048
FLOPS = 2 * K * H * S * 2 + 2 * H * S * V

F32 = mybir.dt.float32
BF16 = mybir.dt.bfloat16
I32 = mybir.dt.int32
U32 = mybir.dt.uint32
U16 = mybir.dt.uint16
U8 = mybir.dt.uint8
FP8X4 = mybir.dt.float8_e4m3fn_x4
ACT = mybir.ActivationFunctionType
ALU = mybir.AluOpType

P = 128
PACK = 4
BLOCK = 128


def tile_picked_zkge_tanh_p_kernel(
    tc, x_words, x_scales, e_words, e_scales, w1, w2, v_words, v_scales, bias, offs, rel, tail, out
):
    nc = tc.nc
    with ExitStack() as ctx:
        keep = ctx.enter_context(tc.tile_pool(name="keep", bufs=1))
        laid = ctx.enter_context(tc.tile_pool(name="laid", bufs=1))
        psum = ctx.enter_context(tc.psum_pool(name="psum", bufs=1))

        def load_list(name, src):
            t = keep.tile([P, src.shape[1]], U16, name=name)
            nc.sync.dma_start(t[:], src)
            return t

        def load_scales(name, src, first):
            t = keep.tile([P, src.shape[2]], U8, name=name, align_bytes=64)
            nc.vector.memset(t[:].bitcast(I32), 0)
            nc.sync.dma_start(t[first : first + 16, :].bitcast(I32), src[0].bitcast(I32))
            return t

        def cleared_plane(name):
            t = keep.tile([P, S], U8, name=name, align_bytes=64)
            nc.vector.memset(t[:].bitcast(I32), 0)
            return t

        def place_scales(plane, picked, first):
            for q in range(4):
                rows = picked[first + 4 * q : first + 4 * q + 4, :]
                nc.sync.dma_start(plane[32 * q : 32 * q + 4, :].bitcast(I32), rows.bitcast(I32))

        def load_words(t, src):
            nc.sync.dma_start(t[:], src[0].rearrange("p n t -> p (n t)").bitcast(I32))

        def load_weight(t, src):
            nc.sync.dma_start(t[:], src.rearrange("(p j) c -> p j c", j=PACK))

        def gather(dst, window, idx):
            nc.vector.tensor_copy(dst, window.indirect(idx))

        def cast_weight(copy, t, raw, m0, m1):
            copy(
                t[:].rearrange("p (t m j) -> p m t j", t=PACK, j=PACK)[:, m0:m1],
                raw[:].rearrange("p j (m t) -> p m t j", t=PACK)[:, m0:m1],
            )

        def quantize(codes, scales, values):
            nc.vector.quantize_mx(out=codes[:].bitcast(FP8X4), scales=scales[:], in_=values[:])
            return codes, scales

        def project(bank, wq, codes, scales, b):
            cols = slice(b * BLOCK, (b + 1) * BLOCK)
            for t in range(PACK):
                chan = slice(t * P, (t + 1) * P)
                nc.tensor.matmul_mx(
                    out=bank[:, t, :],
                    lhsT=wq[0][:, chan].bitcast(FP8X4),
                    lhsT_scale=wq[1][:, chan],
                    rhs=codes[:, cols].bitcast(FP8X4),
                    rhs_scale=scales[:, cols],
                    start=True,
                    stop=True,
                )

        E_ROW, X_ROW, V_ROW = 0, 16, 64

        rel_sb = load_list("rel_sb", rel)
        offs_sb = load_list("offs_sb", offs)
        tail_sb = load_list("tail_sb", tail)
        e_sc = load_scales("e_sc", e_scales, E_ROW)
        x_sc = load_scales("x_sc", x_scales, X_ROW)
        v_sc = load_scales("v_sc", v_scales, V_ROW)
        w2_raw = keep.tile([P, PACK, H], F32, align_bytes=64)
        load_weight(w2_raw, w2)
        e_tab = keep.tile([P, W], I32, align_bytes=64)
        load_words(e_tab, e_words)
        bias_tab = keep.tile([P, G], F32, align_bytes=64)
        nc.vector.memset(bias_tab[:], 0.0)
        nc.sync.dma_start(bias_tab[0:1, :], bias[0:1, :])

        ident = keep.tile([P, P], F32)
        make_identity(nc, ident[:])
        warm = keep.tile([P, 8], F32)
        nc.scalar.activation(warm[64:P, :], bias_tab[64:P, 0:8], ACT.Sigmoid)
        e_plane = cleared_plane("e_plane")
        x_plane = cleared_plane("x_plane")
        v_plane = cleared_plane("v_plane")

        e_s = keep.tile([P, S], U8, align_bytes=64)
        gather(e_s[:], e_sc[:], rel_sb[:])
        place_scales(e_plane, e_s, E_ROW)
        w1_raw = laid.tile([P, PACK, H], F32, offset=0, align_bytes=64)
        load_weight(w1_raw, w1)
        x_tab = keep.tile([P, T], I32, align_bytes=64)
        load_words(x_tab, x_words)
        x_s = keep.tile([P, S], U8, align_bytes=64)
        gather(x_s[:], x_sc[:], offs_sb[:])
        place_scales(x_plane, x_s, X_ROW)
        v_tab = keep.tile([P, G], I32, tag="v_slot", align_bytes=64)
        load_words(v_tab, v_words)
        v_s = keep.tile([P, V], U8, align_bytes=64)
        gather(v_s[:], v_sc[:], tail_sb[:])
        place_scales(v_plane, v_s, V_ROW)

        e_q = keep.tile([P, S], U32, align_bytes=64)
        gather(e_q[:], e_tab[:].bitcast(U32), rel_sb[:])
        w2_bf = keep.tile([P, PACK * H], BF16, align_bytes=64)
        cast_weight(nc.scalar.copy, w2_bf, w2_raw, 0, P)
        w2_codes = keep.tile([P, H], U32, align_bytes=64)
        w2_scales = keep.tile([P, H], U8, align_bytes=64)
        w2_q = quantize(w2_codes, w2_scales, w2_bf)
        bias_row = keep.tile([P, V], F32)
        gather(bias_row[:], bias_tab[:], tail_sb[:])

        ON_VECTOR = 48
        w1_bf = keep.tile([P, PACK * H], BF16, align_bytes=64)
        cast_weight(nc.scalar.copy, w1_bf, w1_raw, ON_VECTOR, P)
        cast_weight(nc.vector.tensor_copy, w1_bf, w1_raw, 0, ON_VECTOR)
        w1_codes = keep.tile([P, H], U32, align_bytes=64)
        w1_scales = keep.tile([P, H], U8, align_bytes=64)
        w1_q = quantize(w1_codes, w1_scales, w1_bf)

        n_blocks = S // BLOCK
        r_sb = []
        for b in range(n_blocks):
            r_bank = psum.tile([P, PACK, BLOCK], F32, name="r_bank", tag="rbank", bufs=4)
            project(r_bank, w2_q, e_q, e_plane, b)
            r_b = laid.tile([P, BLOCK, PACK], F32, name="r%d" % b, offset=b * 4 * BLOCK * PACK, align_bytes=64)
            nc.scalar.activation(r_b[:], r_bank[:].rearrange("p t n -> p n t"), ACT.Tanh)
            r_sb.append(r_b)

        turned = psum.tile([P, V], F32, name="turned", tag="rbank", bufs=4)
        for c in range(V // P):
            nc.tensor.transpose(turned[:, c * P : (c + 1) * P], bias_row[:, c * P : (c + 1) * P], ident[:])
        bias_col = keep.tile([P, V // P], F32)
        nc.scalar.copy(bias_col[:], turned[:, 0:V:P])

        x_q = keep.tile([P, S], U32, align_bytes=64)
        for h in range(2):
            gather(x_q[:, h * S // 2 : (h + 1) * S // 2], x_tab[:].bitcast(U32), offs_sb[:, h * S // 32 : (h + 1) * S // 32])

        def product(b):
            y_bank = psum.tile([P, PACK, BLOCK], F32, name="y_bank", tag="ybank", bufs=3)
            project(y_bank, w1_q, x_q, x_plane, b)
            if b == n_blocks - 1:
                z_b = keep.tile([P, BLOCK * PACK], BF16, name="z_last", tag="v_slot", align_bytes=64)
            else:
                z_b = keep.tile([P, BLOCK * PACK], BF16, name="z%d" % b, align_bytes=64)
            nc.vector.tensor_tensor(
                z_b[:].rearrange("p (n t) -> p n t", t=PACK), y_bank[:].rearrange("p t n -> p n t"), r_sb[b][:], ALU.mult
            )
            return z_b

        def quantize_z(b, z_b):
            z_codes = keep.tile([P, BLOCK], U32, name="z_codes%d" % b, align_bytes=64)
            z_scales = keep.tile([P, BLOCK], U8, name="z_scales%d" % b, align_bytes=64)
            return quantize(z_codes, z_scales, z_b)

        def score(b, z_q, v_q):
            o_bank = psum.tile([P, V], F32, name="o_bank", tag="rbank", bufs=4)
            nc.tensor.matmul_mx(
                out=o_bank[:],
                lhsT=z_q[0][:].bitcast(FP8X4),
                lhsT_scale=z_q[1][:],
                rhs=v_q[:].bitcast(FP8X4),
                rhs_scale=v_plane[:],
                start=True,
                stop=True,
            )
            logit = keep.tile([P, V], F32, name="logit%d" % b)
            prob = keep.tile([P, V], F32, name="prob%d" % b)
            width = V // 2 if b == n_blocks - 1 else V
            for c0 in range(0, V, width):
                cols = slice(c0, c0 + width)
                nc.vector.tensor_tensor(logit[:, cols], o_bank[:, cols], bias_g[:, cols], ALU.add)
                nc.scalar.activation(prob[:, cols], logit[:, cols], ACT.Sigmoid)
                nc.sync.dma_start(out[b * BLOCK : (b + 1) * BLOCK, cols], prob[:, cols])

        z_bf = [product(0)]
        z_qs = []
        for b in range(1, n_blocks - 1):
            z_bf.append(product(b))
            z_qs.append(quantize_z(b - 1, z_bf[b - 1]))
        spread = psum.tile([P, V], F32, name="spread", tag="ybank", bufs=3)
        for c in range(V // P):
            nc.tensor.transpose(spread[:, c * P : (c + 1) * P], bias_col[:, c : c + 1].to_broadcast([P, P]), ident[:])
        bias_g = keep.tile([P, V], F32)
        nc.scalar.copy(bias_g[:], spread[:])
        v_q = keep.tile([P, V], U32, align_bytes=64)
        gather(v_q[:], v_tab[:].bitcast(U32), tail_sb[:])
        z_qs.append(quantize_z(n_blocks - 2, z_bf[n_blocks - 2]))
        z_bf.append(product(n_blocks - 1))
        score(0, z_qs[0], v_q)
        z_qs.append(quantize_z(n_blocks - 1, z_bf[n_blocks - 1]))
        for b in range(1, n_blocks):
            score(b, z_qs[b], v_q)
